import numpy as np
import ml_dtypes


def mxq(x, axis, fmt="e4m3"):
    dtype, down = {"e4m3": (ml_dtypes.float8_e4m3fn, 7), "e5m2": (ml_dtypes.float8_e5m2, 14)}[fmt]
    v = np.moveaxis(np.asarray(x, np.float32).astype(ml_dtypes.bfloat16).astype(np.float64), axis, -1)
    blocks = v.reshape(v.shape[:-1] + (-1, 32))
    amax = np.abs(blocks).max(-1, keepdims=True)
    byte = np.maximum(np.where(amax > 0, np.frexp(amax)[1] - 1 + 127, 0) - down, 1)
    scale = np.exp2(byte - 127.0)
    codes = (blocks / scale).astype(np.float32).astype(dtype).astype(np.float64)
    return np.moveaxis((codes * scale).reshape(v.shape), -1, axis)


WIDE = False


def mx_kscale(k):
    if not WIDE:
        return np.ones(k)
    levels = np.array([10, -10, 5, -5, 0])
    if k % 512:
        return np.exp2(np.random.permutation(np.resize(levels, k // 32))).repeat(32)
    a = np.empty((k // 512, 16))
    for p in range(k // 512):
        a[p, :8] = np.random.permutation(np.resize(levels, 8))
        for g in range(8):
            far = levels[np.abs(levels - a[p, g]) >= 10]
            a[p, g + 8] = far[np.random.randint(len(far))]
    return np.exp2(a.ravel()).repeat(32)


def f64(x):
    return np.asarray(x).astype(np.float64)


def striped(idx):
    return np.tile(idx.reshape(-1, 16).T, (8, 1)).astype(np.uint16)


def unstriped(offs):
    return offs[:16].T.reshape(-1).astype(np.int64)


def striped8(idx):
    return np.concatenate([x.reshape(-1, 16).T for x in idx]).astype(np.uint16)


def runs(offs, k):
    lists = np.stack([offs[16 * r : 16 * r + 16].T.reshape(-1) for r in range(8)]).astype(np.int64)
    return lists[np.arange(k) % 512 // 64]


def pack_weight(w):
    k, n = w.shape
    w = f64(np.asarray(w, np.float32).astype(ml_dtypes.bfloat16)).reshape(k // 32, 32, n)
    amax = np.abs(w).max(1)
    byte = np.clip(np.where(amax > 0, np.frexp(amax)[1] - 1 + 127 - 7, 1), 1, 254)
    scaled = (w * np.exp2(127.0 - byte)[:, None, :]).reshape(k, n).astype(np.float32)
    words = np.ascontiguousarray(scaled.reshape(k // 512, 128, 4, n).transpose(0, 1, 3, 2)).astype(ml_dtypes.float8_e4m3fn).view(np.uint8)
    return words, np.ascontiguousarray(byte.astype(np.uint8).reshape(k // 512, 16, n))


def unpack_weight(words, scales):
    g, p, n, _ = words.shape
    vals = np.ascontiguousarray(words).view(ml_dtypes.float8_e4m3fn).astype(np.float64) * np.repeat(np.exp2(scales.astype(np.float64) - 127.0), 8, axis=1)[..., None]
    return vals.transpose(0, 1, 3, 2).reshape(g * 512, n)


def relu(v):
    return np.maximum(v, 0.0)


def sigmoid(v):
    return 1.0 / (1.0 + np.exp(-np.maximum(v, -700.0)))


K, T, S, V, H, C = 512, 2048, 512, 256, 512, 512


def setup_inputs():
    n = np.random.standard_normal
    s = mx_kscale(K)[:, None]
    packed_xT = pack_weight(n((K, T)) * s)
    perm = np.stack([np.random.permutation(S) for _ in range(8)])
    return {
        "x_words": packed_xT[0],
        "x_scales": packed_xT[1],
        "w1": (n((K, H)) / np.sqrt(K) / s).astype(np.float32),
        "gs": (np.random.uniform(0.5, 1.5, (K, 1)) / s).astype(np.float32),
        "offs": striped(np.random.permutation(T)[:S]),
        "cand": striped(np.random.permutation(T)[:C]),
        "la": striped8(perm[:, :V]),
        "lb": striped8(perm[:, V:]),
    }


def reference(x_words, x_scales, w1, gs, offs, cand, la, lb):
    x_cand = unpack_weight(x_words, x_scales)[:, unstriped(cand)]
    xq = unpack_weight(x_words, x_scales)[:, unstriped(offs)]
    h = relu(mxq(f64(w1), 0, "e4m3").T @ xq)
    z = f64(gs) * h
    s = 0.0625 * ((x_cand.T @ mxq(z, 0, "e4m3")))
    b = s[np.arange(C)[:, None], runs(lb, C)]
    a = s[np.arange(C)[:, None], runs(la, C)]
    t1 = sigmoid(a - b)
    nb = b * (-1.0 * t1 + 1)
    na = a * t1
    sp = np.zeros((C, S))
    sp[np.arange(C)[:, None], runs(la, C)] = na
    out = sp.copy()
    out[np.arange(C)[:, None], runs(lb, C)] = nb
    return out

@@ -1,0 +1,189 @@
+from contextlib import ExitStack
+
+import concourse.mybir as mybir
+
+K, T, S, V, H, C = 512, 2048, 512, 256, 512, 512
+FLOPS = 2 * K * H * S + 2 * K * C * S
+
+F32 = mybir.dt.float32
+BF16 = mybir.dt.bfloat16
+I32 = mybir.dt.int32
+U32 = mybir.dt.uint32
+U16 = mybir.dt.uint16
+U8 = mybir.dt.uint8
+FP8X4 = mybir.dt.float8_e4m3fn_x4
+ALU = mybir.AluOpType
+ACT = mybir.ActivationFunctionType
+
+P = 128
+PACK = 4
+CHUNK = 128
+W_PIECES = [(0, 256), (256, 384), (384, 512)]
+
+
+def tile_picked_candduel_none_p_kernel(tc, x_words, x_scales, w1, gs, offs, cand, la, lb, out):
+    nc = tc.nc
+    with ExitStack() as ctx:
+        keep = ctx.enter_context(tc.tile_pool(name="keep", bufs=1))
+        psum = ctx.enter_context(tc.psum_pool(name="psum", bufs=1))
+
+        offs_sb = keep.tile([P, S // 16], U16, name="offs_sb")
+        cand_sb = keep.tile([P, C // 16], U16, name="cand_sb")
+        la_sb = keep.tile([P, V // 16], U16, name="la_sb")
+        lb_sb = keep.tile([P, V // 16], U16, name="lb_sb")
+        gs_sb = keep.tile([P, PACK], F32, name="gs_sb")
+        table_words = keep.tile([P, T], I32, name="table_words", align_bytes=64)
+        table_scales = keep.tile([P, T], U8, name="table_scales", align_bytes=64)
+
+        nc.vector.memset(table_scales[:, : T // 2].bitcast(I32), 0)
+        nc.gpsimd.memset(table_scales[:, T // 2 :].bitcast(I32), 0)
+        nc.sync.dma_start(offs_sb[:], offs)
+        nc.sync.dma_start(cand_sb[:], cand)
+        for q in range(4):
+            nc.sync.dma_start(table_scales[32 * q : 32 * q + 4, :].bitcast(I32), x_scales[0, 4 * q : 4 * q + 4, :].bitcast(I32))
+        nc.sync.dma_start(table_words[:], x_words[0].rearrange("p n t -> p (n t)").bitcast(I32))
+        w_rows = w1.rearrange("(p j) c -> p j c", j=PACK)
+        w_raw = []
+        for i, (c0, c1) in enumerate(W_PIECES):
+            piece = keep.tile([P, PACK, c1 - c0], F32, name=f"w_raw{i}")
+            nc.sync.dma_start(piece[:], w_rows[:, :, c0:c1])
+            w_raw.append(piece)
+        nc.sync.dma_start(gs_sb[:], gs.rearrange("(p t) o -> p (t o)", t=PACK))
+        nc.sync.dma_start(la_sb[:], la)
+        nc.sync.dma_start(lb_sb[:], lb)
+
+        warm = keep.tile([P, 16], F32, name="warm")
+        nc.gpsimd.memset(warm[:, 0:8], 0.0)
+        nc.scalar.activation(warm[:, 8:16], warm[:, 0:8], ACT.Sigmoid)
+
+        tok_scales = keep.tile([P, S], U8, name="tok_scales", align_bytes=64)
+        nc.vector.tensor_copy(tok_scales[:], table_scales[:].indirect(offs_sb[:]))
+        cand_scales_listed = keep.tile([P, C], U8, name="cand_scales_listed", align_bytes=64)
+        nc.vector.tensor_copy(cand_scales_listed[:], table_scales[:].indirect(cand_sb[:]))
+        tok_words = keep.tile([P, S], U32, name="tok_words", align_bytes=64)
+        nc.vector.tensor_copy(tok_words[:], table_words[:].bitcast(U32).indirect(offs_sb[:]))
+        cand_scales = keep.tile([P, C], U8, name="cand_scales", align_bytes=64)
+        nc.vector.tensor_copy(
+            cand_scales[:].bitcast(I32).rearrange("p (t a) -> p t a", t=PACK),
+            cand_scales_listed[:].bitcast(I32).rearrange("p (a t) -> p t a", t=PACK),
+        )
+        cand_words = keep.tile([P, C], U32, name="cand_words", align_bytes=64)
+        nc.vector.tensor_copy(
+            cand_words[:].rearrange("p (t a c) -> p a t c", t=PACK, c=4),
+            table_words[:].bitcast(U32).indirect(cand_sb[:]),
+        )
+
+        half = P // 2
+        w_bf = [keep.tile([P, PACK, half, PACK], BF16, name=f"w_bf{u}", align_bytes=64) for u in range(2)]
+        w_words = keep.tile([P, H], U32, name="w_words", align_bytes=64)
+        w_scales = keep.tile([P, H], U8, name="w_scales", align_bytes=64)
+
+        def interleave_w(copy, i):
+            c0, c1 = W_PIECES[i]
+            u = c0 // (H // 2)
+            m0, m1 = c0 // PACK - u * half, c1 // PACK - u * half
+            copy(
+                w_bf[u][:, :, m0:m1, :].rearrange("p t m j -> p m j t"),
+                w_raw[i][:].rearrange("p j (m t) -> p m j t", t=PACK),
+            )
+
+        def quantize_w(u):
+            for t in range(PACK):
+                cols = slice(t * P + u * half, t * P + (u + 1) * half)
+                nc.vector.quantize_mx(out=w_words[:, cols].bitcast(FP8X4), scales=w_scales[:, cols], in_=w_bf[u][:, t, :, :].rearrange("p m j -> p (m j)"))
+
+        interleave_w(nc.scalar.copy, 0)
+        interleave_w(nc.scalar.copy, 1)
+        interleave_w(nc.vector.tensor_copy, 2)
+        quantize_w(0)
+        quantize_w(1)
+
+        z_words = keep.tile([P, S], U32, name="z_words", align_bytes=64)
+        z_scales = keep.tile([P, S], U8, name="z_scales", align_bytes=64)
+        n_chunks = S // CHUNK
+        z_bf = [keep.tile([P, CHUNK, PACK], BF16, name=f"z_bf{i}", align_bytes=64) for i in range(n_chunks)]
+
+        def hidden(i):
+            cols = slice(i * CHUNK, (i + 1) * CHUNK)
+            bank = psum.tile([P, PACK, CHUNK], F32, name=f"h_bank{i}", tag=f"bank{i}")
+            for t in range(PACK):
+                nc.tensor.matmul_mx(
+                    out=bank[:, t, :],
+                    lhsT=w_words[:, t * P : (t + 1) * P].bitcast(FP8X4),
+                    lhsT_scale=w_scales[:, t * P : (t + 1) * P],
+                    rhs=tok_words[:, cols].bitcast(FP8X4),
+                    rhs_scale=tok_scales[:, cols],
+                    start=True,
+                    stop=True,
+                )
+            nc.vector.scalar_tensor_tensor(
+                out=z_bf[i][:],
+                in0=bank[:].rearrange("p t n -> p n t"),
+                scalar=0.0,
+                in1=gs_sb[:].unsqueeze(1).to_broadcast([P, CHUNK, PACK]),
+                op0=ALU.max,
+                op1=ALU.mult,
+            )
+
+        def quantize_z(i):
+            cols = slice(i * CHUNK, (i + 1) * CHUNK)
+            nc.vector.quantize_mx(out=z_words[:, cols].bitcast(FP8X4), scales=z_scales[:, cols], in_=z_bf[i][:].rearrange("p n t -> p (n t)"))
+
+        hidden(0)
+        for i in range(1, n_chunks):
+            hidden(i)
+            quantize_z(i - 1)
+        quantize_z(n_chunks - 1)
+
+        def scores(t, dst, c0, c1, widths, tag):
+            bank = psum.tile([P, S], F32, name=f"s_bank{t}_{c0}", tag=tag)
+            a0 = c0
+            for width in widths:
+                nc.tensor.matmul_mx(
+                    out=bank[:, a0 : a0 + width],
+                    lhsT=cand_words[:, t * P : (t + 1) * P].bitcast(FP8X4),
+                    lhsT_scale=cand_scales[:, t * P : (t + 1) * P],
+                    rhs=z_words[:, a0 : a0 + width].bitcast(FP8X4),
+                    rhs_scale=z_scales[:, a0 : a0 + width],
+                    start=True,
+                    stop=True,
+                )
+                a0 = a0 + width
+            nc.scalar.activation(dst[:, c0:c1], bank[:, c0:c1], ACT.Copy, scale=0.0625)
+
+        s_sb = [keep.tile([P, S], F32, name=f"s_sb{t}") for t in range(PACK)]
+        scores(0, s_sb[0], 0, 384, [256, 128], "bank4")
+        scores(0, s_sb[0], 384, 512, [128], "bank5")
+        scores(1, s_sb[1], 0, 512, [512], "bank6")
+        scores(2, s_sb[2], 0, 512, [512], "bank7")
+        scores(3, s_sb[3], 0, 512, [512], "bank0")
+
+        a_sb = [keep.tile([P, V], F32, name=f"a_sb{t}") for t in range(PACK)]
+        b_sb = [keep.tile([P, V], F32, name=f"b_sb{t}") for t in range(PACK)]
+        keep_a = [keep.tile([P, V], F32, name=f"keep_a{t}") for t in range(PACK)]
+        keep_b = [keep.tile([P, V], F32, name=f"keep_b{t}") for t in range(PACK)]
+
+        def fetch(t):
+            nc.vector.tensor_copy(a_sb[t][:], s_sb[t][:].indirect(la_sb[:]))
+            nc.vector.tensor_copy(b_sb[t][:], s_sb[t][:].indirect(lb_sb[:]))
+
+        def gates(t):
+            diff = keep.tile([P, V], F32, name=f"diff{t}")
+            nc.vector.tensor_tensor(diff[:], a_sb[t][:], b_sb[t][:], ALU.subtract)
+            nc.scalar.activation(keep_a[t][:], diff[:], ACT.Sigmoid)
+            nc.scalar.activation(keep_b[t][:], diff[:], ACT.Sigmoid, scale=-1.0)
+
+        fetch(0)
+        for t in range(1, PACK):
+            fetch(t)
+            gates(t - 1)
+        gates(PACK - 1)
+
+        out_rows = out.rearrange("(a t c) n -> t a c n", t=PACK, c=4)
+        res = [keep.tile([P, S], F32, name=f"res{t}") for t in range(PACK)]
+        for pair in ((0, 1), (2, 3)):
+            for t in pair:
+                nc.vector.tensor_tensor(res[t][:].indirect(la_sb[:]), a_sb[t][:], keep_a[t][:], ALU.mult)
+            for t in pair:
+                nc.vector.tensor_tensor(res[t][:].indirect(lb_sb[:]), b_sb[t][:], keep_b[t][:], ALU.mult)
+                nc.sync.dma_start(out_rows[t], res[t][:])

@@ -1,6 +1,7 @@
 from contextlib import ExitStack
 
 import concourse.mybir as mybir
+from concourse.masks import make_identity
 
 K, T, S, V, H, C = 512, 2048, 512, 256, 512, 512
 FLOPS = 2 * K * H * S + 2 * K * C * S
@@ -18,7 +19,7 @@ ACT = mybir.ActivationFunctionType
 P = 128
 PACK = 4
 CHUNK = 128
-W_PIECES = [(0, 256), (256, 384), (384, 512)]
+W_PIECES = [(0, 128), (128, 256), (256, 384), (384, 512)]
 
 
 def tile_picked_candduel_none_p_kernel(tc, x_words, x_scales, w1, gs, offs, cand, la, lb, out):
@@ -56,12 +57,15 @@ def tile_picked_candduel_none_p_kernel(tc, x_words, x_scales, w1, gs, offs, cand
         nc.gpsimd.memset(warm[:, 0:8], 0.0)
         nc.scalar.activation(warm[:, 8:16], warm[:, 0:8], ACT.Sigmoid)
 
+        ident = keep.tile([P, P], F32, name="ident")
+        make_identity(nc, ident[:])
+
         tok_scales = keep.tile([P, S], U8, name="tok_scales", align_bytes=64)
         nc.vector.tensor_copy(tok_scales[:], table_scales[:].indirect(offs_sb[:]))
         cand_scales_listed = keep.tile([P, C], U8, name="cand_scales_listed", align_bytes=64)
         nc.vector.tensor_copy(cand_scales_listed[:], table_scales[:].indirect(cand_sb[:]))
-        tok_words = keep.tile([P, S], U32, name="tok_words", align_bytes=64)
-        nc.vector.tensor_copy(tok_words[:], table_words[:].bitcast(U32).indirect(offs_sb[:]))
+        tok_words_early = keep.tile([P, S // 2], U32, name="tok_words_early", align_bytes=64)
+        nc.vector.tensor_copy(tok_words_early[:], table_words[:].bitcast(U32).indirect(offs_sb[:, : S // 32]))
         cand_scales = keep.tile([P, C], U8, name="cand_scales", align_bytes=64)
         nc.vector.tensor_copy(
             cand_scales[:].bitcast(I32).rearrange("p (t a) -> p t a", t=PACK),
@@ -74,7 +78,7 @@ def tile_picked_candduel_none_p_kernel(tc, x_words, x_scales, w1, gs, offs, cand
         )
 
         half = P // 2
-        w_bf = [keep.tile([P, PACK, half, PACK], BF16, name=f"w_bf{u}", align_bytes=64) for u in range(2)]
+        w_bf = [keep.tile([P, PACK, half, PACK], BF16, name=f"w_bf{u}", tag=f"w_bf{u}", align_bytes=64) for u in range(2)]
         w_words = keep.tile([P, H], U32, name="w_words", align_bytes=64)
         w_scales = keep.tile([P, H], U8, name="w_scales", align_bytes=64)
 
@@ -94,9 +98,13 @@ def tile_picked_candduel_none_p_kernel(tc, x_words, x_scales, w1, gs, offs, cand
 
         interleave_w(nc.scalar.copy, 0)
         interleave_w(nc.scalar.copy, 1)
-        interleave_w(nc.vector.tensor_copy, 2)
+        interleave_w(nc.scalar.copy, 2)
         quantize_w(0)
+        interleave_w(nc.vector.tensor_copy, 3)
         quantize_w(1)
+        tok_words_late = keep.tile([P, S // 2], U32, name="tok_words_late", tag="w_bf1", align_bytes=64)
+        nc.vector.tensor_copy(tok_words_late[:], table_words[:].bitcast(U32).indirect(offs_sb[:, S // 32 :]))
+        tok_words = [tok_words_early, tok_words_late]
 
         z_words = keep.tile([P, S], U32, name="z_words", align_bytes=64)
         z_scales = keep.tile([P, S], U8, name="z_scales", align_bytes=64)
@@ -111,7 +119,7 @@ def tile_picked_candduel_none_p_kernel(tc, x_words, x_scales, w1, gs, offs, cand
                     out=bank[:, t, :],
                     lhsT=w_words[:, t * P : (t + 1) * P].bitcast(FP8X4),
                     lhsT_scale=w_scales[:, t * P : (t + 1) * P],
-                    rhs=tok_words[:, cols].bitcast(FP8X4),
+                    rhs=tok_words[i // 2][:, (i % 2) * CHUNK : (i % 2 + 1) * CHUNK].bitcast(FP8X4),
                     rhs_scale=tok_scales[:, cols],
                     start=True,
                     stop=True,
@@ -152,38 +160,50 @@ def tile_picked_candduel_none_p_kernel(tc, x_words, x_scales, w1, gs, offs, cand
             nc.scalar.activation(dst[:, c0:c1], bank[:, c0:c1], ACT.Copy, scale=0.0625)
 
         s_sb = [keep.tile([P, S], F32, name=f"s_sb{t}") for t in range(PACK)]
-        scores(0, s_sb[0], 0, 384, [256, 128], "bank4")
-        scores(0, s_sb[0], 384, 512, [128], "bank5")
+        scores(0, s_sb[0], 0, 256, [256], "bank4")
+        scores(0, s_sb[0], 256, 384, [128], "bank5")
+        scores(0, s_sb[0], 384, 512, [128], "bank0")
         scores(1, s_sb[1], 0, 512, [512], "bank6")
         scores(2, s_sb[2], 0, 512, [512], "bank7")
-        scores(3, s_sb[3], 0, 512, [512], "bank0")
+        scores(3, s_sb[3], 0, 512, [512], "bank3")
 
         a_sb = [keep.tile([P, V], F32, name=f"a_sb{t}") for t in range(PACK)]
         b_sb = [keep.tile([P, V], F32, name=f"b_sb{t}") for t in range(PACK)]
-        keep_a = [keep.tile([P, V], F32, name=f"keep_a{t}") for t in range(PACK)]
-        keep_b = [keep.tile([P, V], F32, name=f"keep_b{t}") for t in range(PACK)]
+        keep_a2 = [keep.tile([P, 2 * V], F32, name=f"keep_a{u}") for u in range(2)]
+        keep_b2 = [keep.tile([P, 2 * V], F32, name=f"keep_b{u}") for u in range(2)]
+        keep_a = [keep_a2[t // 2][:, (t % 2) * V : (t % 2 + 1) * V] for t in range(PACK)]
+        keep_b = [keep_b2[t // 2][:, (t % 2) * V : (t % 2 + 1) * V] for t in range(PACK)]
 
         def fetch(t):
             nc.vector.tensor_copy(a_sb[t][:], s_sb[t][:].indirect(la_sb[:]))
-            nc.vector.tensor_copy(b_sb[t][:], s_sb[t][:].indirect(lb_sb[:]))
+            nc.vector.tensor_scalar(b_sb[t][:], s_sb[t][:].indirect(lb_sb[:]), -1.0, 0.0, ALU.mult, ALU.add)
 
         def gates(t):
-            diff = keep.tile([P, V], F32, name=f"diff{t}")
-            nc.vector.tensor_tensor(diff[:], a_sb[t][:], b_sb[t][:], ALU.subtract)
-            nc.scalar.activation(keep_a[t][:], diff[:], ACT.Sigmoid)
-            nc.scalar.activation(keep_b[t][:], diff[:], ACT.Sigmoid, scale=-1.0)
+            diff_turned = psum.tile([P, V], F32, name=f"diff_turned{t}", tag=f"bank{1 + t % 2}")
+            for u in range(V // P):
+                cols = slice(u * P, (u + 1) * P)
+                nc.tensor.matmul(diff_turned[:, cols], lhsT=a_sb[t][:, cols], rhs=ident[:], start=True, stop=False, is_transpose=True)
+                nc.tensor.matmul(diff_turned[:, cols], lhsT=b_sb[t][:, cols], rhs=ident[:], start=False, stop=True, is_transpose=True)
+            gate_turned = keep.tile([P, V], F32, name=f"gate_turned{t}")
+            nc.scalar.activation(gate_turned[:], diff_turned[:], ACT.Sigmoid)
+            gate = psum.tile([P, V], F32, name=f"gate{t}", tag=f"bank{1 + (t + 1) % 2}")
+            for u in range(V // P):
+                cols = slice(u * P, (u + 1) * P)
+                nc.tensor.transpose(gate[:, cols], gate_turned[:, cols], ident[:])
+            nc.scalar.copy(keep_a[t], gate[:])
+            if t % 2 == 1:
+                nc.scalar.activation(keep_b2[t // 2][:], keep_a2[t // 2][:], ACT.Copy, bias=-1.0)
 
-        fetch(0)
-        for t in range(1, PACK):
+        for t in range(PACK):
             fetch(t)
-            gates(t - 1)
-        gates(PACK - 1)
+        for t in range(PACK):
+            gates(t)
 
         out_rows = out.rearrange("(a t c) n -> t a c n", t=PACK, c=4)
         res = [keep.tile([P, S], F32, name=f"res{t}") for t in range(PACK)]
         for pair in ((0, 1), (2, 3)):
             for t in pair:
-                nc.vector.tensor_tensor(res[t][:].indirect(la_sb[:]), a_sb[t][:], keep_a[t][:], ALU.mult)
+                nc.vector.tensor_tensor(res[t][:].indirect(la_sb[:]), a_sb[t][:], keep_a[t], ALU.mult)
             for t in pair:
-                nc.vector.tensor_tensor(res[t][:].indirect(lb_sb[:]), b_sb[t][:], keep_b[t][:], ALU.mult)
+                nc.vector.tensor_tensor(res[t][:].indirect(lb_sb[:]), b_sb[t][:], keep_b[t], ALU.mult)
                 nc.sync.dma_start(out_rows[t], res[t][:])

@@ -36,8 +36,7 @@ def tile_picked_candduel_none_p_kernel(tc, x_words, x_scales, w1, gs, offs, cand
         table_words = keep.tile([P, T], I32, name="table_words", align_bytes=64)
         table_scales = keep.tile([P, T], U8, name="table_scales", align_bytes=64)
 
-        nc.vector.memset(table_scales[:, : T // 2].bitcast(I32), 0)
-        nc.gpsimd.memset(table_scales[:, T // 2 :].bitcast(I32), 0)
+        nc.vector.memset(table_scales[:].bitcast(I32), 0)
         nc.sync.dma_start(offs_sb[:], offs)
         nc.sync.dma_start(cand_sb[:], cand)
         for q in range(4):
@@ -54,11 +53,12 @@ def tile_picked_candduel_none_p_kernel(tc, x_words, x_scales, w1, gs, offs, cand
         nc.sync.dma_start(lb_sb[:], lb)
 
         warm = keep.tile([P, 16], F32, name="warm")
-        nc.gpsimd.memset(warm[:, 0:8], 0.0)
+        nc.vector.memset(warm[:, 0:8], 0.0)
         nc.scalar.activation(warm[:, 8:16], warm[:, 0:8], ACT.Sigmoid)
 
         ident = keep.tile([P, P], F32, name="ident")
-        make_identity(nc, ident[:])
+        nc.vector.memset(ident[:], 0.0)
+        make_identity(nc, ident[:], nomemset=True)
 
         tok_scales = keep.tile([P, S], U8, name="tok_scales", align_bytes=64)
         nc.vector.tensor_copy(tok_scales[:], table_scales[:].indirect(offs_sb[:]))
@@ -87,8 +87,8 @@ def tile_picked_candduel_none_p_kernel(tc, x_words, x_scales, w1, gs, offs, cand
             u = c0 // (H // 2)
             m0, m1 = c0 // PACK - u * half, c1 // PACK - u * half
             copy(
-                w_bf[u][:, :, m0:m1, :].rearrange("p t m j -> p m j t"),
-                w_raw[i][:].rearrange("p j (m t) -> p m j t", t=PACK),
+                w_bf[u][:, :, m0:m1, :].rearrange("p t m j -> p m t j"),
+                w_raw[i][:].rearrange("p j (m t) -> p m t j", t=PACK),
             )
 
         def quantize_w(u):
@@ -179,14 +179,14 @@ def tile_picked_candduel_none_p_kernel(tc, x_words, x_scales, w1, gs, offs, cand
             nc.vector.tensor_scalar(b_sb[t][:], s_sb[t][:].indirect(lb_sb[:]), -1.0, 0.0, ALU.mult, ALU.add)
 
         def gates(t):
-            diff_turned = psum.tile([P, V], F32, name=f"diff_turned{t}", tag=f"bank{1 + t % 2}")
+            diff_turned = psum.tile([P, V], F32, name=f"diff_turned{t}", tag=f"bank{(1, 2, 4, 5)[t]}")
             for u in range(V // P):
                 cols = slice(u * P, (u + 1) * P)
                 nc.tensor.matmul(diff_turned[:, cols], lhsT=a_sb[t][:, cols], rhs=ident[:], start=True, stop=False, is_transpose=True)
                 nc.tensor.matmul(diff_turned[:, cols], lhsT=b_sb[t][:, cols], rhs=ident[:], start=False, stop=True, is_transpose=True)
             gate_turned = keep.tile([P, V], F32, name=f"gate_turned{t}")
             nc.scalar.activation(gate_turned[:], diff_turned[:], ACT.Sigmoid)
-            gate = psum.tile([P, V], F32, name=f"gate{t}", tag=f"bank{1 + (t + 1) % 2}")
+            gate = psum.tile([P, V], F32, name=f"gate{t}", tag=f"bank{(4, 5, 1, 2)[t]}")
             for u in range(V // P):
                 cols = slice(u * P, (u + 1) * P)
                 nc.tensor.transpose(gate[:, cols], gate_turned[:, cols], ident[:])

@@ -40,7 +40,8 @@ def tile_picked_candduel_none_p_kernel(tc, x_words, x_scales, w1, gs, offs, cand
         nc.sync.dma_start(offs_sb[:], offs)
         nc.sync.dma_start(cand_sb[:], cand)
         for q in range(4):
-            nc.sync.dma_start(table_scales[32 * q : 32 * q + 4, :].bitcast(I32), x_scales[0, 4 * q : 4 * q + 4, :].bitcast(I32))
+            queue = nc.sync if q % 2 == 0 else nc.scalar
+            queue.dma_start(table_scales[32 * q : 32 * q + 4, :].bitcast(I32), x_scales[0, 4 * q : 4 * q + 4, :].bitcast(I32))
         nc.sync.dma_start(table_words[:], x_words[0].rearrange("p n t -> p (n t)").bitcast(I32))
         w_rows = w1.rearrange("(p j) c -> p j c", j=PACK)
         w_raw = []
@@ -51,10 +52,6 @@ def tile_picked_candduel_none_p_kernel(tc, x_words, x_scales, w1, gs, offs, cand
         nc.sync.dma_start(gs_sb[:], gs.rearrange("(p t) o -> p (t o)", t=PACK))
         nc.sync.dma_start(la_sb[:], la)
         nc.sync.dma_start(lb_sb[:], lb)
-
-        warm = keep.tile([P, 16], F32, name="warm")
-        nc.vector.memset(warm[:, 0:8], 0.0)
-        nc.scalar.activation(warm[:, 8:16], warm[:, 0:8], ACT.Sigmoid)
 
         ident = keep.tile([P, P], F32, name="ident")
         nc.vector.memset(ident[:], 0.0)
@@ -100,7 +97,7 @@ def tile_picked_candduel_none_p_kernel(tc, x_words, x_scales, w1, gs, offs, cand
         interleave_w(nc.scalar.copy, 1)
         interleave_w(nc.scalar.copy, 2)
         quantize_w(0)
-        interleave_w(nc.vector.tensor_copy, 3)
+        interleave_w(nc.scalar.copy, 3)
         quantize_w(1)
         tok_words_late = keep.tile([P, S // 2], U32, name="tok_words_late", tag="w_bf1", align_bytes=64)
         nc.vector.tensor_copy(tok_words_late[:], table_words[:].bitcast(U32).indirect(offs_sb[:, S // 32 :]))
@@ -185,12 +182,12 @@ def tile_picked_candduel_none_p_kernel(tc, x_words, x_scales, w1, gs, offs, cand
                 nc.tensor.matmul(diff_turned[:, cols], lhsT=a_sb[t][:, cols], rhs=ident[:], start=True, stop=False, is_transpose=True)
                 nc.tensor.matmul(diff_turned[:, cols], lhsT=b_sb[t][:, cols], rhs=ident[:], start=False, stop=True, is_transpose=True)
             gate_turned = keep.tile([P, V], F32, name=f"gate_turned{t}")
-            nc.scalar.activation(gate_turned[:], diff_turned[:], ACT.Sigmoid)
+            nc.scalar.activation(gate_turned[:], diff_turned[:], ACT.Tanh, scale=0.5)
             gate = psum.tile([P, V], F32, name=f"gate{t}", tag=f"bank{(4, 5, 1, 2)[t]}")
             for u in range(V // P):
                 cols = slice(u * P, (u + 1) * P)
                 nc.tensor.transpose(gate[:, cols], gate_turned[:, cols], ident[:])
-            nc.scalar.copy(keep_a[t], gate[:])
+            nc.scalar.activation(keep_a[t], gate[:], ACT.Copy, scale=0.5, bias=0.5)
             if t % 2 == 1:
                 nc.scalar.activation(keep_b2[t // 2][:], keep_a2[t // 2][:], ACT.Copy, bias=-1.0)
 

@@ -79,13 +79,13 @@ def tile_picked_candduel_none_p_kernel(tc, x_words, x_scales, w1, gs, offs, cand
         w_words = keep.tile([P, H], U32, name="w_words", align_bytes=64)
         w_scales = keep.tile([P, H], U8, name="w_scales", align_bytes=64)
 
-        def interleave_w(copy, i):
+        def interleave_w(copy, i, tiles):
             c0, c1 = W_PIECES[i]
             u = c0 // (H // 2)
             m0, m1 = c0 // PACK - u * half, c1 // PACK - u * half
             copy(
-                w_bf[u][:, :, m0:m1, :].rearrange("p t m j -> p m t j"),
-                w_raw[i][:].rearrange("p j (m t) -> p m t j", t=PACK),
+                w_bf[u][:, tiles, m0:m1, :].rearrange("p t m j -> p m t j"),
+                w_raw[i][:].rearrange("p j (m t) -> p m t j", t=PACK)[:, :, tiles, :],
             )
 
         def quantize_w(u):
@@ -93,11 +93,12 @@ def tile_picked_candduel_none_p_kernel(tc, x_words, x_scales, w1, gs, offs, cand
                 cols = slice(t * P + u * half, t * P + (u + 1) * half)
                 nc.vector.quantize_mx(out=w_words[:, cols].bitcast(FP8X4), scales=w_scales[:, cols], in_=w_bf[u][:, t, :, :].rearrange("p m j -> p (m j)"))
 
-        interleave_w(nc.scalar.copy, 0)
-        interleave_w(nc.scalar.copy, 1)
-        interleave_w(nc.scalar.copy, 2)
+        interleave_w(nc.scalar.copy, 0, slice(0, 4))
+        interleave_w(nc.scalar.copy, 1, slice(0, 4))
+        interleave_w(nc.scalar.copy, 2, slice(0, 4))
         quantize_w(0)
-        interleave_w(nc.scalar.copy, 3)
+        interleave_w(nc.vector.tensor_copy, 3, slice(0, 2))
+        interleave_w(nc.vector.tensor_copy, 3, slice(2, 4))
         quantize_w(1)
         tok_words_late = keep.tile([P, S // 2], U32, name="tok_words_late", tag="w_bf1", align_bytes=64)
         nc.vector.tensor_copy(tok_words_late[:], table_words[:].bitcast(U32).indirect(offs_sb[:, S // 32 :]))

from contextlib import ExitStack

import concourse.mybir as mybir
from concourse.masks import make_identity

K, T, S, V, H, C = 512, 2048, 512, 256, 512, 512
FLOPS = 2 * K * H * S + 2 * K * C * S

F32 = mybir.dt.float32
BF16 = mybir.dt.bfloat16
I32 = mybir.dt.int32
U32 = mybir.dt.uint32
U16 = mybir.dt.uint16
U8 = mybir.dt.uint8
FP8X4 = mybir.dt.float8_e4m3fn_x4
ALU = mybir.AluOpType
ACT = mybir.ActivationFunctionType

P = 128
PACK = 4
CHUNK = 128
W_PIECES = [(0, 128), (128, 256), (256, 384), (384, 512)]


def tile_picked_candduel_none_p_kernel(tc, x_words, x_scales, w1, gs, offs, cand, la, lb, out):
    nc = tc.nc
    with ExitStack() as ctx:
        keep = ctx.enter_context(tc.tile_pool(name="keep", bufs=1))
        psum = ctx.enter_context(tc.psum_pool(name="psum", bufs=1))

        offs_sb = keep.tile([P, S // 16], U16, name="offs_sb")
        cand_sb = keep.tile([P, C // 16], U16, name="cand_sb")
        la_sb = keep.tile([P, V // 16], U16, name="la_sb")
        lb_sb = keep.tile([P, V // 16], U16, name="lb_sb")
        gs_sb = keep.tile([P, PACK], F32, name="gs_sb")
        table_words = keep.tile([P, T], I32, name="table_words", align_bytes=64)
        table_scales = keep.tile([P, T], U8, name="table_scales", align_bytes=64)

        nc.vector.memset(table_scales[:].bitcast(I32), 0)
        nc.sync.dma_start(offs_sb[:], offs)
        nc.sync.dma_start(cand_sb[:], cand)
        for q in range(4):
            queue = nc.sync if q % 2 == 0 else nc.scalar
            queue.dma_start(table_scales[32 * q : 32 * q + 4, :].bitcast(I32), x_scales[0, 4 * q : 4 * q + 4, :].bitcast(I32))
        nc.sync.dma_start(table_words[:], x_words[0].rearrange("p n t -> p (n t)").bitcast(I32))
        w_rows = w1.rearrange("(p j) c -> p j c", j=PACK)
        w_raw = []
        for i, (c0, c1) in enumerate(W_PIECES):
            piece = keep.tile([P, PACK, c1 - c0], F32, name=f"w_raw{i}")
            nc.sync.dma_start(piece[:], w_rows[:, :, c0:c1])
            w_raw.append(piece)
        nc.sync.dma_start(gs_sb[:], gs.rearrange("(p t) o -> p (t o)", t=PACK))
        nc.sync.dma_start(la_sb[:], la)
        nc.sync.dma_start(lb_sb[:], lb)

        ident = keep.tile([P, P], F32, name="ident")
        nc.vector.memset(ident[:], 0.0)
        make_identity(nc, ident[:], nomemset=True)

        tok_scales = keep.tile([P, S], U8, name="tok_scales", align_bytes=64)
        nc.vector.tensor_copy(tok_scales[:], table_scales[:].indirect(offs_sb[:]))
        cand_scales_listed = keep.tile([P, C], U8, name="cand_scales_listed", align_bytes=64)
        nc.vector.tensor_copy(cand_scales_listed[:], table_scales[:].indirect(cand_sb[:]))
        tok_words_early = keep.tile([P, S // 2], U32, name="tok_words_early", align_bytes=64)
        nc.vector.tensor_copy(tok_words_early[:], table_words[:].bitcast(U32).indirect(offs_sb[:, : S // 32]))
        cand_scales = keep.tile([P, C], U8, name="cand_scales", align_bytes=64)
        nc.vector.tensor_copy(
            cand_scales[:].bitcast(I32).rearrange("p (t a) -> p t a", t=PACK),
            cand_scales_listed[:].bitcast(I32).rearrange("p (a t) -> p t a", t=PACK),
        )
        cand_words = keep.tile([P, C], U32, name="cand_words", align_bytes=64)
        nc.vector.tensor_copy(
            cand_words[:].rearrange("p (t a c) -> p a t c", t=PACK, c=4),
            table_words[:].bitcast(U32).indirect(cand_sb[:]),
        )

        half = P // 2
        w_bf = [keep.tile([P, PACK, half, PACK], BF16, name=f"w_bf{u}", tag=f"w_bf{u}", align_bytes=64) for u in range(2)]
        w_words = keep.tile([P, H], U32, name="w_words", align_bytes=64)
        w_scales = keep.tile([P, H], U8, name="w_scales", align_bytes=64)

        def interleave_w(copy, i, tiles):
            c0, c1 = W_PIECES[i]
            u = c0 // (H // 2)
            m0, m1 = c0 // PACK - u * half, c1 // PACK - u * half
            copy(
                w_bf[u][:, tiles, m0:m1, :].rearrange("p t m j -> p m t j"),
                w_raw[i][:].rearrange("p j (m t) -> p m t j", t=PACK)[:, :, tiles, :],
            )

        def quantize_w(u):
            for t in range(PACK):
                cols = slice(t * P + u * half, t * P + (u + 1) * half)
                nc.vector.quantize_mx(out=w_words[:, cols].bitcast(FP8X4), scales=w_scales[:, cols], in_=w_bf[u][:, t, :, :].rearrange("p m j -> p (m j)"))

        interleave_w(nc.scalar.copy, 0, slice(0, 4))
        interleave_w(nc.scalar.copy, 1, slice(0, 4))
        interleave_w(nc.scalar.copy, 2, slice(0, 4))
        quantize_w(0)
        interleave_w(nc.vector.tensor_copy, 3, slice(0, 2))
        interleave_w(nc.vector.tensor_copy, 3, slice(2, 4))
        quantize_w(1)
        tok_words_late = keep.tile([P, S // 2], U32, name="tok_words_late", tag="w_bf1", align_bytes=64)
        nc.vector.tensor_copy(tok_words_late[:], table_words[:].bitcast(U32).indirect(offs_sb[:, S // 32 :]))
        tok_words = [tok_words_early, tok_words_late]

        z_words = keep.tile([P, S], U32, name="z_words", align_bytes=64)
        z_scales = keep.tile([P, S], U8, name="z_scales", align_bytes=64)
        n_chunks = S // CHUNK
        z_bf = [keep.tile([P, CHUNK, PACK], BF16, name=f"z_bf{i}", align_bytes=64) for i in range(n_chunks)]

        def hidden(i):
            cols = slice(i * CHUNK, (i + 1) * CHUNK)
            bank = psum.tile([P, PACK, CHUNK], F32, name=f"h_bank{i}", tag=f"bank{i}")
            for t in range(PACK):
                nc.tensor.matmul_mx(
                    out=bank[:, t, :],
                    lhsT=w_words[:, t * P : (t + 1) * P].bitcast(FP8X4),
                    lhsT_scale=w_scales[:, t * P : (t + 1) * P],
                    rhs=tok_words[i // 2][:, (i % 2) * CHUNK : (i % 2 + 1) * CHUNK].bitcast(FP8X4),
                    rhs_scale=tok_scales[:, cols],
                    start=True,
                    stop=True,
                )
            nc.vector.scalar_tensor_tensor(
                out=z_bf[i][:],
                in0=bank[:].rearrange("p t n -> p n t"),
                scalar=0.0,
                in1=gs_sb[:].unsqueeze(1).to_broadcast([P, CHUNK, PACK]),
                op0=ALU.max,
                op1=ALU.mult,
            )

        def quantize_z(i):
            cols = slice(i * CHUNK, (i + 1) * CHUNK)
            nc.vector.quantize_mx(out=z_words[:, cols].bitcast(FP8X4), scales=z_scales[:, cols], in_=z_bf[i][:].rearrange("p n t -> p (n t)"))

        hidden(0)
        for i in range(1, n_chunks):
            hidden(i)
            quantize_z(i - 1)
        quantize_z(n_chunks - 1)

        def scores(t, dst, c0, c1, widths, tag):
            bank = psum.tile([P, S], F32, name=f"s_bank{t}_{c0}", tag=tag)
            a0 = c0
            for width in widths:
                nc.tensor.matmul_mx(
                    out=bank[:, a0 : a0 + width],
                    lhsT=cand_words[:, t * P : (t + 1) * P].bitcast(FP8X4),
                    lhsT_scale=cand_scales[:, t * P : (t + 1) * P],
                    rhs=z_words[:, a0 : a0 + width].bitcast(FP8X4),
                    rhs_scale=z_scales[:, a0 : a0 + width],
                    start=True,
                    stop=True,
                )
                a0 = a0 + width
            nc.scalar.activation(dst[:, c0:c1], bank[:, c0:c1], ACT.Copy, scale=0.0625)

        s_sb = [keep.tile([P, S], F32, name=f"s_sb{t}") for t in range(PACK)]
        scores(0, s_sb[0], 0, 256, [256], "bank4")
        scores(0, s_sb[0], 256, 384, [128], "bank5")
        scores(0, s_sb[0], 384, 512, [128], "bank0")
        scores(1, s_sb[1], 0, 512, [512], "bank6")
        scores(2, s_sb[2], 0, 512, [512], "bank7")
        scores(3, s_sb[3], 0, 512, [512], "bank3")

        a_sb = [keep.tile([P, V], F32, name=f"a_sb{t}") for t in range(PACK)]
        b_sb = [keep.tile([P, V], F32, name=f"b_sb{t}") for t in range(PACK)]
        keep_a2 = [keep.tile([P, 2 * V], F32, name=f"keep_a{u}") for u in range(2)]
        keep_b2 = [keep.tile([P, 2 * V], F32, name=f"keep_b{u}") for u in range(2)]
        keep_a = [keep_a2[t // 2][:, (t % 2) * V : (t % 2 + 1) * V] for t in range(PACK)]
        keep_b = [keep_b2[t // 2][:, (t % 2) * V : (t % 2 + 1) * V] for t in range(PACK)]

        def fetch(t):
            nc.vector.tensor_copy(a_sb[t][:], s_sb[t][:].indirect(la_sb[:]))
            nc.vector.tensor_scalar(b_sb[t][:], s_sb[t][:].indirect(lb_sb[:]), -1.0, 0.0, ALU.mult, ALU.add)

        def gates(t):
            diff_turned = psum.tile([P, V], F32, name=f"diff_turned{t}", tag=f"bank{(1, 2, 4, 5)[t]}")
            for u in range(V // P):
                cols = slice(u * P, (u + 1) * P)
                nc.tensor.matmul(diff_turned[:, cols], lhsT=a_sb[t][:, cols], rhs=ident[:], start=True, stop=False, is_transpose=True)
                nc.tensor.matmul(diff_turned[:, cols], lhsT=b_sb[t][:, cols], rhs=ident[:], start=False, stop=True, is_transpose=True)
            gate_turned = keep.tile([P, V], F32, name=f"gate_turned{t}")
            nc.scalar.activation(gate_turned[:], diff_turned[:], ACT.Tanh, scale=0.5)
            gate = psum.tile([P, V], F32, name=f"gate{t}", tag=f"bank{(4, 5, 1, 2)[t]}")
            for u in range(V // P):
                cols = slice(u * P, (u + 1) * P)
                nc.tensor.transpose(gate[:, cols], gate_turned[:, cols], ident[:])
            nc.scalar.activation(keep_a[t], gate[:], ACT.Copy, scale=0.5, bias=0.5)
            if t % 2 == 1:
                nc.scalar.activation(keep_b2[t // 2][:], keep_a2[t // 2][:], ACT.Copy, bias=-1.0)

        for t in range(PACK):
            fetch(t)
        for t in range(PACK):
            gates(t)

        out_rows = out.rearrange("(a t c) n -> t a c n", t=PACK, c=4)
        res = [keep.tile([P, S], F32, name=f"res{t}") for t in range(PACK)]
        for pair in ((0, 1), (2, 3)):
            for t in pair:
                nc.vector.tensor_tensor(res[t][:].indirect(la_sb[:]), a_sb[t][:], keep_a[t], ALU.mult)
            for t in pair:
                nc.vector.tensor_tensor(res[t][:].indirect(lb_sb[:]), b_sb[t][:], keep_b[t], ALU.mult)
                nc.sync.dma_start(out_rows[t], res[t][:])
